import numpy as np
import ml_dtypes


def mxq(x, axis, fmt="e4m3"):
    dtype, down = {"e4m3": (ml_dtypes.float8_e4m3fn, 7), "e5m2": (ml_dtypes.float8_e5m2, 14)}[fmt]
    v = np.moveaxis(np.asarray(x, np.float32).astype(ml_dtypes.bfloat16).astype(np.float64), axis, -1)
    blocks = v.reshape(v.shape[:-1] + (-1, 32))
    amax = np.abs(blocks).max(-1, keepdims=True)
    byte = np.maximum(np.where(amax > 0, np.frexp(amax)[1] - 1 + 127, 0) - down, 1)
    scale = np.exp2(byte - 127.0)
    codes = (blocks / scale).astype(np.float32).astype(dtype).astype(np.float64)
    return np.moveaxis((codes * scale).reshape(v.shape), -1, axis)


WIDE = False


def mx_kscale(k):
    if not WIDE:
        return np.ones(k)
    levels = np.array([10, -10, 5, -5, 0])
    if k % 512:
        return np.exp2(np.random.permutation(np.resize(levels, k // 32))).repeat(32)
    a = np.empty((k // 512, 16))
    for p in range(k // 512):
        a[p, :8] = np.random.permutation(np.resize(levels, 8))
        for g in range(8):
            far = levels[np.abs(levels - a[p, g]) >= 10]
            a[p, g + 8] = far[np.random.randint(len(far))]
    return np.exp2(a.ravel()).repeat(32)


def f64(x):
    return np.asarray(x).astype(np.float64)


def striped8(idx):
    return np.concatenate([v.reshape(-1, 16).T for v in idx]).astype(np.uint16)


def unstriped8(offs):
    return np.stack([offs[16 * g:16 * g + 16].T.reshape(-1) for g in range(8)]).astype(np.int64)


E2M1 = np.array([0.0, 0.5, 1.0, 1.5, 2.0, 3.0, 4.0, 6.0, -0.0, -0.5, -1.0, -1.5, -2.0, -3.0, -4.0, -6.0])


def pack_weight(w, fmt):
    k, n = w.shape
    w = f64(np.asarray(w, np.float32).astype(ml_dtypes.bfloat16)).reshape(k // 32, 32, n)
    amax = np.abs(w).max(1)
    if fmt == "e4m3":
        byte = np.frexp(amax)[1] - 1 + 127 - 7
    else:
        mant, ex = np.frexp(amax / 6.0)
        byte = np.where(mant > 0.5, ex, ex - 1) + 127
    byte = np.clip(np.where(amax > 0, byte, 1), 1, 254)
    scaled = (w * np.exp2(127.0 - byte)[:, None, :]).reshape(k, n).astype(np.float32)
    by_word = np.ascontiguousarray(scaled.reshape(k // 512, 128, 4, n).transpose(0, 1, 3, 2))
    if fmt == "e4m3":
        words = by_word.astype(ml_dtypes.float8_e4m3fn).view(np.uint8)
    else:
        c = by_word.astype(ml_dtypes.float4_e2m1fn).view(np.uint8) & 0xF
        words = (c[..., 0::2] | (c[..., 1::2] << 4)).reshape(k // 512, 128, 2 * n)
    return np.ascontiguousarray(words), np.ascontiguousarray(byte.astype(np.uint8).reshape(k // 512, 16, n))


def unpack_weight(words, scales, fmt):
    g, _, n = scales.shape
    words = np.ascontiguousarray(words).reshape(g, 128, n, -1)
    if fmt == "e4m3":
        vals = words.view(ml_dtypes.float8_e4m3fn).astype(np.float64)
    else:
        nib = np.empty((g, 128, n, 4), np.uint8)
        nib[..., 0::2] = words & 0xF
        nib[..., 1::2] = words >> 4
        vals = E2M1[nib]
    vals = vals * np.repeat(np.exp2(scales.astype(np.float64) - 127.0), 8, axis=1)[..., None]
    return vals.transpose(0, 1, 3, 2).reshape(g * 512, n)


K, M, T, S = 512, 1024, 2048, 512


def setup_inputs():
    n = np.random.standard_normal
    s = mx_kscale(K)[:, None]
    p_w = pack_weight(n((K, M)) / np.sqrt(K) / s, "e2m1")
    return {
        "xT": (n((K, T)) * s).astype(np.float32),
        "w_words": p_w[0],
        "w_scales": p_w[1],
        "wgt": np.repeat(np.random.uniform(0.5, 2.0, (8, S)), 16, axis=0).astype(np.float32),
        "offs": striped8(np.stack([np.random.permutation(T)[:S] for _ in range(8)])),
    }


def reference(xT, w_words, w_scales, wgt, offs):
    idx = unstriped8(offs)
    group = np.arange(K) % 512 // 64
    xg = f64(wgt)[np.arange(K) // 4 % 128] * f64(xT)[np.arange(K)[:, None], idx[group]]
    xT_ = mxq(xg, 0, "e4m3")
    w_ = unpack_weight(w_words, w_scales, "e2m1")
    y = w_.T @ xT_
    return y

@@ -1,0 +1,133 @@
+from contextlib import ExitStack
+
+import concourse.mybir as mybir
+
+F32 = mybir.dt.float32
+BF16 = mybir.dt.bfloat16
+I32 = mybir.dt.int32
+U32 = mybir.dt.uint32
+U16 = mybir.dt.uint16
+U8 = mybir.dt.uint8
+FP8X4 = mybir.dt.float8_e4m3fn_x4
+FP4X4 = mybir.dt.float4_e2m1fn_x4
+MULT = mybir.AluOpType.mult
+
+P = 128
+K, M, T, S = 512, 1024, 2048, 512
+HALF = 256
+FLOPS = 2 * K * M * S
+
+
+def tile_list_heads_none_kernel(tc, xT, w_words, w_scales, wgt, offs, out):
+    nc = tc.nc
+    with ExitStack() as ctx:
+        keep = ctx.enter_context(tc.tile_pool(name="keep", bufs=1))
+        psum = ctx.enter_context(tc.psum_pool(name="psum", bufs=1))
+
+        offsets = keep.tile([P, S // 16], U16, name="offsets")
+        nc.sync.dma_start(offsets[:], offs)
+        weight = keep.tile([P, S], F32, name="weight")
+        nc.scalar.dma_start(weight[:], wgt)
+        planes = []
+        for i in range(4):
+            plane = keep.tile([P, T], F32, name=f"plane{i}")
+            nc.sync.dma_start(plane[:], xT.rearrange("(p i) t -> i p t", i=4)[i])
+            planes.append(plane)
+        w_codes = keep.tile([P, 2 * M], U8, name="w_codes", align_bytes=64)
+        nc.sync.dma_start(w_codes[:].bitcast(I32), w_words[0].bitcast(I32))
+        w_scale = keep.tile([P, M], U8, name="w_scale", align_bytes=64)
+        nc.vector.memset(w_scale[:].bitcast(I32), 0)
+        for q in range(4):
+            nc.scalar.dma_start(w_scale[32 * q : 32 * q + 4, :].bitcast(I32), w_scales[0, 4 * q : 4 * q + 4, :].bitcast(I32))
+
+        gathered = []
+        mixed = []
+        codes = []
+        scales = []
+        for c in range(2):
+            g = keep.tile([P, 4, HALF], F32, name=f"gathered{c}")
+            b = keep.tile([P, HALF, 4], BF16, name=f"mixed{c}", align_bytes=64)
+            x = keep.tile([P, HALF], U32, name=f"codes{c}", align_bytes=64)
+            s = keep.tile([P, HALF], U8, name=f"scales{c}", align_bytes=64)
+            gathered.append(g)
+            mixed.append(b)
+            codes.append(x)
+            scales.append(s)
+
+        def gather(i, c):
+            nc.vector.tensor_tensor(
+                gathered[c][:, i, :],
+                planes[i][:].indirect(offsets[:, 16 * c : 16 * c + 16]),
+                weight[:, HALF * c : HALF * c + HALF],
+                MULT,
+            )
+
+        def interleave(engine_copy, c, pair, lo, hi):
+            engine_copy(
+                mixed[c][:, lo:hi, 2 * pair : 2 * pair + 2],
+                gathered[c][:, 2 * pair : 2 * pair + 2, lo:hi].rearrange("p t n -> p n t"),
+            )
+
+        def quantize(c):
+            nc.vector.quantize_mx(
+                out=codes[c][:].bitcast(FP8X4),
+                scales=scales[c][:],
+                in_=mixed[c][:].rearrange("p n t -> p (n t)"),
+            )
+
+        def multiply(c, m, acc):
+            nc.tensor.matmul_mx(
+                out=acc,
+                lhsT=w_codes[:, 256 * m : 256 * m + 256].bitcast(FP4X4),
+                lhsT_scale=w_scale[:, P * m : P * m + P],
+                rhs=codes[c][:].bitcast(FP8X4),
+                rhs_scale=scales[c][:],
+                start=True,
+                stop=True,
+            )
+
+        for i in range(4):
+            for c in range(2):
+                gather(i, c)
+            if i == 1:
+                for c in range(2):
+                    interleave(nc.scalar.copy, c, 0, 0, HALF)
+
+        def bank(name):
+            acc = psum.tile([P, 2, HALF], F32, name=name)
+            return acc
+
+        first = [bank("first0"), bank("first1")]
+        both = [bank(f"both{j}") for j in range(4)]
+        last = [bank("last0"), bank("last1")]
+
+        def pair_rows(m):
+            return out[P * m : P * m + 2 * P, :].rearrange("(u p) n -> p u n", u=2)
+
+        interleave(nc.scalar.copy, 0, 1, 0, 128)
+        interleave(nc.vector.tensor_copy, 0, 1, 128, 256)
+        quantize(0)
+        for m in range(4):
+            multiply(0, m, first[m // 2][:, m % 2, :])
+        for m in range(4):
+            row = keep.tile([P, HALF], F32, name=f"row{m}")
+            nc.scalar.copy(row[:], first[m // 2][:, m % 2, :])
+            nc.sync.dma_start(out[P * m : P * m + P, 0:HALF], row[:])
+        for m in range(4):
+            multiply(0, 4 + m, both[m][:, 0, :])
+        interleave(nc.vector.tensor_copy, 1, 1, 0, HALF)
+        quantize(1)
+        for m in range(4):
+            multiply(1, 4 + m, both[m][:, 1, :])
+        for m in range(4):
+            multiply(1, m, last[m // 2][:, m % 2, :])
+        for m in range(4):
+            full = keep.tile([P, S], F32, name=f"full{m}")
+            copy = nc.vector.tensor_copy if m % 2 == 0 else nc.scalar.copy
+            copy(full[:], both[m][:].rearrange("p u n -> p (u n)"))
+            nc.sync.dma_start(out[P * (4 + m) : P * (5 + m), :], full[:])
+        for j in range(2):
+            tail = keep.tile([P, 2, HALF], F32, name=f"tail{j}")
+            copy = nc.vector.tensor_copy if j == 0 else nc.scalar.copy
+            copy(tail[:], last[j][:])
+            nc.sync.dma_start(pair_rows(2 * j)[:, :, HALF:S], tail[:])

@@ -14,7 +14,6 @@ MULT = mybir.AluOpType.mult
 
 P = 128
 K, M, T, S = 512, 1024, 2048, 512
-HALF = 256
 FLOPS = 2 * K * M * S
 
 
@@ -24,10 +23,14 @@ def tile_list_heads_none_kernel(tc, xT, w_words, w_scales, wgt, offs, out):
         keep = ctx.enter_context(tc.tile_pool(name="keep", bufs=1))
         psum = ctx.enter_context(tc.psum_pool(name="psum", bufs=1))
 
+        w_pack = keep.tile([P, 32], F32, name="w_pack", align_bytes=64)
+        w_turned = keep.tile([P, 32], F32, name="w_turned", align_bytes=64)
+        w_spread = keep.tile([P, S], F32, name="w_spread", align_bytes=64)
+        weight = keep.tile([P, S], F32, name="weight", align_bytes=64)
+        nc.scalar.dma_start(w_pack[:], wgt.rearrange("(g r) (s c) -> r g s c", r=16, c=32)[0])
+
         offsets = keep.tile([P, S // 16], U16, name="offsets")
         nc.sync.dma_start(offsets[:], offs)
-        weight = keep.tile([P, S], F32, name="weight")
-        nc.scalar.dma_start(weight[:], wgt)
         planes = []
         for i in range(4):
             plane = keep.tile([P, T], F32, name=f"plane{i}")
@@ -40,94 +43,108 @@ def tile_list_heads_none_kernel(tc, xT, w_words, w_scales, wgt, offs, out):
         for q in range(4):
             nc.scalar.dma_start(w_scale[32 * q : 32 * q + 4, :].bitcast(I32), w_scales[0, 4 * q : 4 * q + 4, :].bitcast(I32))
 
-        gathered = []
-        mixed = []
-        codes = []
-        scales = []
-        for c in range(2):
-            g = keep.tile([P, 4, HALF], F32, name=f"gathered{c}")
-            b = keep.tile([P, HALF, 4], BF16, name=f"mixed{c}", align_bytes=64)
-            x = keep.tile([P, HALF], U32, name=f"codes{c}", align_bytes=64)
-            s = keep.tile([P, HALF], U8, name=f"scales{c}", align_bytes=64)
-            gathered.append(g)
-            mixed.append(b)
-            codes.append(x)
-            scales.append(s)
+        nc.vector.transpose(w_turned[:], w_pack[:])
+        for h in range(2):
+            nc.vector.tensor_copy(
+                w_spread[:, 256 * h : 256 * h + 256].rearrange("p (s u r) -> p s u r", u=2, r=16),
+                w_turned[:].rearrange("p (u s) -> p s u", u=2)[:, 8 * h : 8 * h + 8, :].unsqueeze(3).to_broadcast([P, 8, 2, 16]),
+            )
+        for h in range(2):
+            nc.vector.transpose(weight[:, 256 * h : 256 * h + 256], w_spread[:, 256 * h : 256 * h + 256])
 
-        def gather(i, c):
+        gathered = keep.tile([P, 4, S], F32, name="gathered")
+        mixed = keep.tile([P, S, 4], BF16, name="mixed", align_bytes=64)
+        codes = keep.tile([P, S], U32, name="codes", align_bytes=64)
+        scales = keep.tile([P, S], U8, name="scales", align_bytes=64)
+
+        def gather(i, lo, hi):
             nc.vector.tensor_tensor(
-                gathered[c][:, i, :],
-                planes[i][:].indirect(offsets[:, 16 * c : 16 * c + 16]),
-                weight[:, HALF * c : HALF * c + HALF],
+                gathered[:, i, lo:hi],
+                planes[i][:].indirect(offsets[:, lo // 16 : hi // 16]),
+                weight[:, lo:hi],
                 MULT,
             )
 
-        def interleave(engine_copy, c, pair, lo, hi):
+        def interleave(engine_copy, pair, lo, hi):
             engine_copy(
-                mixed[c][:, lo:hi, 2 * pair : 2 * pair + 2],
-                gathered[c][:, 2 * pair : 2 * pair + 2, lo:hi].rearrange("p t n -> p n t"),
+                mixed[:, lo:hi, 2 * pair : 2 * pair + 2],
+                gathered[:, 2 * pair : 2 * pair + 2, lo:hi].rearrange("p t n -> p n t"),
             )
 
-        def quantize(c):
+        def quantize(lo, hi):
             nc.vector.quantize_mx(
-                out=codes[c][:].bitcast(FP8X4),
-                scales=scales[c][:],
-                in_=mixed[c][:].rearrange("p n t -> p (n t)"),
+                out=codes[:, lo:hi].bitcast(FP8X4),
+                scales=scales[:, lo:hi],
+                in_=mixed[:, lo:hi, :].rearrange("p n t -> p (n t)"),
             )
 
-        def multiply(c, m, acc):
+        acc = []
+        for m in range(8):
+            bank = psum.tile([P, S], F32, name=f"bank{m}")
+            acc.append(bank)
+
+        def multiply(m, lo, hi):
             nc.tensor.matmul_mx(
-                out=acc,
+                out=acc[m][:, lo:hi],
                 lhsT=w_codes[:, 256 * m : 256 * m + 256].bitcast(FP4X4),
                 lhsT_scale=w_scale[:, P * m : P * m + P],
-                rhs=codes[c][:].bitcast(FP8X4),
-                rhs_scale=scales[c][:],
+                rhs=codes[:, lo:hi].bitcast(FP8X4),
+                rhs_scale=scales[:, lo:hi],
                 start=True,
                 stop=True,
             )
 
-        for i in range(4):
-            for c in range(2):
-                gather(i, c)
+        def finish(engine_copy, m, lo, hi):
+            row = keep.tile([P, hi - lo], F32, name=f"row{m}_{lo}")
+            engine_copy(row[:], acc[m][:, lo:hi])
+            nc.sync.dma_start(out[P * m : P * m + P, lo:hi], row[:])
+
+        vec, act = nc.vector.tensor_copy, nc.scalar.copy
+        for i in range(3):
+            for lo in (0, 256):
+                gather(i, lo, lo + 256)
             if i == 1:
-                for c in range(2):
-                    interleave(nc.scalar.copy, c, 0, 0, HALF)
+                for lo in (0, 256):
+                    interleave(act, 0, lo, lo + 256)
 
-        def bank(name):
-            acc = psum.tile([P, 2, HALF], F32, name=name)
-            return acc
-
-        first = [bank("first0"), bank("first1")]
-        both = [bank(f"both{j}") for j in range(4)]
-        last = [bank("last0"), bank("last1")]
-
-        def pair_rows(m):
-            return out[P * m : P * m + 2 * P, :].rearrange("(u p) n -> p u n", u=2)
-
-        interleave(nc.scalar.copy, 0, 1, 0, 128)
-        interleave(nc.vector.tensor_copy, 0, 1, 128, 256)
-        quantize(0)
-        for m in range(4):
-            multiply(0, m, first[m // 2][:, m % 2, :])
-        for m in range(4):
-            row = keep.tile([P, HALF], F32, name=f"row{m}")
-            nc.scalar.copy(row[:], first[m // 2][:, m % 2, :])
-            nc.sync.dma_start(out[P * m : P * m + P, 0:HALF], row[:])
-        for m in range(4):
-            multiply(0, 4 + m, both[m][:, 0, :])
-        interleave(nc.vector.tensor_copy, 1, 1, 0, HALF)
-        quantize(1)
-        for m in range(4):
-            multiply(1, 4 + m, both[m][:, 1, :])
-        for m in range(4):
-            multiply(1, m, last[m // 2][:, m % 2, :])
-        for m in range(4):
-            full = keep.tile([P, S], F32, name=f"full{m}")
-            copy = nc.vector.tensor_copy if m % 2 == 0 else nc.scalar.copy
-            copy(full[:], both[m][:].rearrange("p u n -> p (u n)"))
-            nc.sync.dma_start(out[P * (4 + m) : P * (5 + m), :], full[:])
-        for j in range(2):
-            tail = keep.tile([P, 2, HALF], F32, name=f"tail{j}")
-            copy = nc.vector.tensor_copy if j == 0 else nc.scalar.copy
-            copy(tail[:], last[j][:])
-            nc.sync.dma_start(pair_rows(2 * j)[:, :, HALF:S], tail[:])
+        gather(3, 0, 128)
+        gather(3, 128, 256)
+        interleave(act, 1, 0, 128)
+        quantize(0, 128)
+        multiply(0, 0, 128)
+        multiply(1, 0, 128)
+        gather(3, 256, 384)
+        interleave(act, 1, 128, 256)
+        quantize(128, 256)
+        gather(3, 384, 512)
+        interleave(act, 1, 256, 384)
+        interleave(act, 1, 384, 512)
+        finish(act, 0, 0, 128)
+        finish(vec, 1, 0, 128)
+        multiply(2, 0, 256)
+        multiply(3, 0, 256)
+        quantize(256, 512)
+        finish(act, 2, 0, 256)
+        finish(vec, 3, 0, 256)
+        multiply(0, 128, 256)
+        multiply(0, 256, 512)
+        finish(act, 0, 128, 512)
+        multiply(1, 128, 256)
+        multiply(1, 256, 512)
+        finish(vec, 1, 128, 512)
+        multiply(2, 256, 512)
+        finish(act, 2, 256, 512)
+        multiply(3, 256, 512)
+        finish(vec, 3, 256, 512)
+        multiply(4, 0, 256)
+        multiply(4, 256, 512)
+        finish(act, 4, 0, 512)
+        multiply(5, 0, 256)
+        multiply(5, 256, 512)
+        finish(vec, 5, 0, 512)
+        multiply(6, 0, 256)
+        multiply(6, 256, 512)
+        finish(act, 6, 0, 512)
+        multiply(7, 0, 256)
+        multiply(7, 256, 512)
+        finish(vec, 7, 0, 512)

@@ -27,7 +27,7 @@ def tile_list_heads_none_kernel(tc, xT, w_words, w_scales, wgt, offs, out):
         w_turned = keep.tile([P, 32], F32, name="w_turned", align_bytes=64)
         w_spread = keep.tile([P, S], F32, name="w_spread", align_bytes=64)
         weight = keep.tile([P, S], F32, name="weight", align_bytes=64)
-        nc.scalar.dma_start(w_pack[:], wgt.rearrange("(g r) (s c) -> r g s c", r=16, c=32)[0])
+        nc.sync.dma_start(w_pack[:], wgt.rearrange("(g r) (s c) -> r g s c", r=16, c=32)[0])
 
         offsets = keep.tile([P, S // 16], U16, name="offsets")
         nc.sync.dma_start(offsets[:], offs)
@@ -41,7 +41,7 @@ def tile_list_heads_none_kernel(tc, xT, w_words, w_scales, wgt, offs, out):
         w_scale = keep.tile([P, M], U8, name="w_scale", align_bytes=64)
         nc.vector.memset(w_scale[:].bitcast(I32), 0)
         for q in range(4):
-            nc.scalar.dma_start(w_scale[32 * q : 32 * q + 4, :].bitcast(I32), w_scales[0, 4 * q : 4 * q + 4, :].bitcast(I32))
+            nc.sync.dma_start(w_scale[32 * q : 32 * q + 4, :].bitcast(I32), w_scales[0, 4 * q : 4 * q + 4, :].bitcast(I32))
 
         nc.vector.transpose(w_turned[:], w_pack[:])
         for h in range(2):
@@ -113,25 +113,27 @@ def tile_list_heads_none_kernel(tc, xT, w_words, w_scales, wgt, offs, out):
         quantize(0, 128)
         multiply(0, 0, 128)
         multiply(1, 0, 128)
+        multiply(2, 0, 128)
+        multiply(3, 0, 128)
         gather(3, 256, 384)
         interleave(act, 1, 128, 256)
         quantize(128, 256)
         gather(3, 384, 512)
         interleave(act, 1, 256, 384)
         interleave(act, 1, 384, 512)
-        finish(act, 0, 0, 128)
-        finish(vec, 1, 0, 128)
-        multiply(2, 0, 256)
-        multiply(3, 0, 256)
+        multiply(0, 128, 256)
+        multiply(1, 128, 256)
+        multiply(2, 128, 256)
+        multiply(3, 128, 256)
         quantize(256, 512)
+        finish(act, 0, 0, 256)
+        finish(vec, 1, 0, 256)
         finish(act, 2, 0, 256)
         finish(vec, 3, 0, 256)
-        multiply(0, 128, 256)
         multiply(0, 256, 512)
-        finish(act, 0, 128, 512)
-        multiply(1, 128, 256)
+        finish(act, 0, 256, 512)
         multiply(1, 256, 512)
-        finish(vec, 1, 128, 512)
+        finish(vec, 1, 256, 512)
         multiply(2, 256, 512)
         finish(act, 2, 256, 512)
         multiply(3, 256, 512)

from contextlib import ExitStack

import concourse.mybir as mybir

F32 = mybir.dt.float32
BF16 = mybir.dt.bfloat16
I32 = mybir.dt.int32
U32 = mybir.dt.uint32
U16 = mybir.dt.uint16
U8 = mybir.dt.uint8
FP8X4 = mybir.dt.float8_e4m3fn_x4
FP4X4 = mybir.dt.float4_e2m1fn_x4
MULT = mybir.AluOpType.mult

P = 128
K, M, T, S = 512, 1024, 2048, 512
FLOPS = 2 * K * M * S


def tile_list_heads_none_kernel(tc, xT, w_words, w_scales, wgt, offs, out):
    nc = tc.nc
    with ExitStack() as ctx:
        keep = ctx.enter_context(tc.tile_pool(name="keep", bufs=1))
        psum = ctx.enter_context(tc.psum_pool(name="psum", bufs=1))

        w_pack = keep.tile([P, 32], F32, name="w_pack", align_bytes=64)
        w_turned = keep.tile([P, 32], F32, name="w_turned", align_bytes=64)
        w_spread = keep.tile([P, S], F32, name="w_spread", align_bytes=64)
        weight = keep.tile([P, S], F32, name="weight", align_bytes=64)
        nc.sync.dma_start(w_pack[:], wgt.rearrange("(g r) (s c) -> r g s c", r=16, c=32)[0])

        offsets = keep.tile([P, S // 16], U16, name="offsets")
        nc.sync.dma_start(offsets[:], offs)
        planes = []
        for i in range(4):
            plane = keep.tile([P, T], F32, name=f"plane{i}")
            nc.sync.dma_start(plane[:], xT.rearrange("(p i) t -> i p t", i=4)[i])
            planes.append(plane)
        w_codes = keep.tile([P, 2 * M], U8, name="w_codes", align_bytes=64)
        nc.sync.dma_start(w_codes[:].bitcast(I32), w_words[0].bitcast(I32))
        w_scale = keep.tile([P, M], U8, name="w_scale", align_bytes=64)
        nc.vector.memset(w_scale[:].bitcast(I32), 0)
        for q in range(4):
            nc.sync.dma_start(w_scale[32 * q : 32 * q + 4, :].bitcast(I32), w_scales[0, 4 * q : 4 * q + 4, :].bitcast(I32))

        nc.vector.transpose(w_turned[:], w_pack[:])
        for h in range(2):
            nc.vector.tensor_copy(
                w_spread[:, 256 * h : 256 * h + 256].rearrange("p (s u r) -> p s u r", u=2, r=16),
                w_turned[:].rearrange("p (u s) -> p s u", u=2)[:, 8 * h : 8 * h + 8, :].unsqueeze(3).to_broadcast([P, 8, 2, 16]),
            )
        for h in range(2):
            nc.vector.transpose(weight[:, 256 * h : 256 * h + 256], w_spread[:, 256 * h : 256 * h + 256])

        gathered = keep.tile([P, 4, S], F32, name="gathered")
        mixed = keep.tile([P, S, 4], BF16, name="mixed", align_bytes=64)
        codes = keep.tile([P, S], U32, name="codes", align_bytes=64)
        scales = keep.tile([P, S], U8, name="scales", align_bytes=64)

        def gather(i, lo, hi):
            nc.vector.tensor_tensor(
                gathered[:, i, lo:hi],
                planes[i][:].indirect(offsets[:, lo // 16 : hi // 16]),
                weight[:, lo:hi],
                MULT,
            )

        def interleave(engine_copy, pair, lo, hi):
            engine_copy(
                mixed[:, lo:hi, 2 * pair : 2 * pair + 2],
                gathered[:, 2 * pair : 2 * pair + 2, lo:hi].rearrange("p t n -> p n t"),
            )

        def quantize(lo, hi):
            nc.vector.quantize_mx(
                out=codes[:, lo:hi].bitcast(FP8X4),
                scales=scales[:, lo:hi],
                in_=mixed[:, lo:hi, :].rearrange("p n t -> p (n t)"),
            )

        acc = []
        for m in range(8):
            bank = psum.tile([P, S], F32, name=f"bank{m}")
            acc.append(bank)

        def multiply(m, lo, hi):
            nc.tensor.matmul_mx(
                out=acc[m][:, lo:hi],
                lhsT=w_codes[:, 256 * m : 256 * m + 256].bitcast(FP4X4),
                lhsT_scale=w_scale[:, P * m : P * m + P],
                rhs=codes[:, lo:hi].bitcast(FP8X4),
                rhs_scale=scales[:, lo:hi],
                start=True,
                stop=True,
            )

        def finish(engine_copy, m, lo, hi):
            row = keep.tile([P, hi - lo], F32, name=f"row{m}_{lo}")
            engine_copy(row[:], acc[m][:, lo:hi])
            nc.sync.dma_start(out[P * m : P * m + P, lo:hi], row[:])

        vec, act = nc.vector.tensor_copy, nc.scalar.copy
        for i in range(3):
            for lo in (0, 256):
                gather(i, lo, lo + 256)
            if i == 1:
                for lo in (0, 256):
                    interleave(act, 0, lo, lo + 256)

        gather(3, 0, 128)
        gather(3, 128, 256)
        interleave(act, 1, 0, 128)
        quantize(0, 128)
        multiply(0, 0, 128)
        multiply(1, 0, 128)
        multiply(2, 0, 128)
        multiply(3, 0, 128)
        gather(3, 256, 384)
        interleave(act, 1, 128, 256)
        quantize(128, 256)
        gather(3, 384, 512)
        interleave(act, 1, 256, 384)
        interleave(act, 1, 384, 512)
        multiply(0, 128, 256)
        multiply(1, 128, 256)
        multiply(2, 128, 256)
        multiply(3, 128, 256)
        quantize(256, 512)
        finish(act, 0, 0, 256)
        finish(vec, 1, 0, 256)
        finish(act, 2, 0, 256)
        finish(vec, 3, 0, 256)
        multiply(0, 256, 512)
        finish(act, 0, 256, 512)
        multiply(1, 256, 512)
        finish(vec, 1, 256, 512)
        multiply(2, 256, 512)
        finish(act, 2, 256, 512)
        multiply(3, 256, 512)
        finish(vec, 3, 256, 512)
        multiply(4, 0, 256)
        multiply(4, 256, 512)
        finish(act, 4, 0, 512)
        multiply(5, 0, 256)
        multiply(5, 256, 512)
        finish(vec, 5, 0, 512)
        multiply(6, 0, 256)
        multiply(6, 256, 512)
        finish(act, 6, 0, 512)
        multiply(7, 0, 256)
        multiply(7, 256, 512)
        finish(vec, 7, 0, 512)
